import numpy as np
import ml_dtypes


def mxq(x, axis, fmt="e4m3"):
    dtype, down = {"e4m3": (ml_dtypes.float8_e4m3fn, 7), "e5m2": (ml_dtypes.float8_e5m2, 14)}[fmt]
    v = np.moveaxis(np.asarray(x, np.float32).astype(ml_dtypes.bfloat16).astype(np.float64), axis, -1)
    blocks = v.reshape(v.shape[:-1] + (-1, 32))
    amax = np.abs(blocks).max(-1, keepdims=True)
    byte = np.maximum(np.where(amax > 0, np.frexp(amax)[1] - 1 + 127, 0) - down, 1)
    scale = np.exp2(byte - 127.0)
    codes = (blocks / scale).astype(np.float32).astype(dtype).astype(np.float64)
    return np.moveaxis((codes * scale).reshape(v.shape), -1, axis)


WIDE = False


def mx_kscale(k):
    if not WIDE:
        return np.ones(k)
    levels = np.array([10, -10, 5, -5, 0])
    if k % 512:
        return np.exp2(np.random.permutation(np.resize(levels, k // 32))).repeat(32)
    a = np.empty((k // 512, 16))
    for p in range(k // 512):
        a[p, :8] = np.random.permutation(np.resize(levels, 8))
        for g in range(8):
            far = levels[np.abs(levels - a[p, g]) >= 10]
            a[p, g + 8] = far[np.random.randint(len(far))]
    return np.exp2(a.ravel()).repeat(32)


def f64(x):
    return np.asarray(x).astype(np.float64)


def striped(idx):
    return np.tile(idx.reshape(-1, 16).T, (8, 1)).astype(np.uint16)


def unstriped(offs):
    return offs[:16].T.reshape(-1).astype(np.int64)


E2M1 = np.array([0.0, 0.5, 1.0, 1.5, 2.0, 3.0, 4.0, 6.0, -0.0, -0.5, -1.0, -1.5, -2.0, -3.0, -4.0, -6.0])


def pack_weight(w, fmt):
    k, n = w.shape
    w = f64(np.asarray(w, np.float32).astype(ml_dtypes.bfloat16)).reshape(k // 32, 32, n)
    amax = np.abs(w).max(1)
    if fmt == "e4m3":
        byte = np.frexp(amax)[1] - 1 + 127 - 7
    else:
        mant, ex = np.frexp(amax / 6.0)
        byte = np.where(mant > 0.5, ex, ex - 1) + 127
    byte = np.clip(np.where(amax > 0, byte, 1), 1, 254)
    scaled = (w * np.exp2(127.0 - byte)[:, None, :]).reshape(k, n).astype(np.float32)
    by_word = np.ascontiguousarray(scaled.reshape(k // 512, 128, 4, n).transpose(0, 1, 3, 2))
    if fmt == "e4m3":
        words = by_word.astype(ml_dtypes.float8_e4m3fn).view(np.uint8)
    else:
        c = by_word.astype(ml_dtypes.float4_e2m1fn).view(np.uint8) & 0xF
        words = (c[..., 0::2] | (c[..., 1::2] << 4)).reshape(k // 512, 128, 2 * n)
    return np.ascontiguousarray(words), np.ascontiguousarray(byte.astype(np.uint8).reshape(k // 512, 16, n))


def unpack_weight(words, scales, fmt):
    g, _, n = scales.shape
    words = np.ascontiguousarray(words).reshape(g, 128, n, -1)
    if fmt == "e4m3":
        vals = words.view(ml_dtypes.float8_e4m3fn).astype(np.float64)
    else:
        nib = np.empty((g, 128, n, 4), np.uint8)
        nib[..., 0::2] = words & 0xF
        nib[..., 1::2] = words >> 4
        vals = E2M1[nib]
    vals = vals * np.repeat(np.exp2(scales.astype(np.float64) - 127.0), 8, axis=1)[..., None]
    return vals.transpose(0, 1, 3, 2).reshape(g * 512, n)


def gelu(v):
    return 0.5 * v * (1.0 + np.tanh(np.sqrt(2.0 / np.pi) * (v + 0.044715 * v**3)))


K, T, E, C, H, N = 512, 512, 16, 128, 512, 384
TOP = 4


def by_expert(wq, xq):
    return np.concatenate([wq[e].T @ xq[:, e * C:(e + 1) * C] for e in range(E)], axis=1)


def setup_inputs():
    n = np.random.standard_normal
    s = mx_kscale(K)[:, None]
    u = mx_kscale(H)
    deal = np.repeat(np.arange(E), C).reshape(TOP, T)[:, np.random.permutation(T)]
    deal = np.take_along_axis(deal, np.argsort(np.random.rand(TOP, T), axis=0), axis=0)
    for _ in range(8):
        s_, t_ = np.random.permutation(T).reshape(2, -1); r = np.random.randint(TOP, size=T // 2); x, y = deal[r, s_].copy(), deal[r, t_].copy()
        ok = ~((deal[:, s_] == y).any(0) | (deal[:, t_] == x).any(0)); deal[r[ok], s_[ok]] = y[ok]; deal[r[ok], t_[ok]] = x[ok]
    order = np.lexsort((np.random.rand(TOP * T), deal.reshape(-1)))
    slot_token = order % T; pos = np.empty(TOP * T, np.int64); pos[order] = np.arange(TOP * T); pos = pos.reshape(TOP, T)
    g = np.random.uniform(0.5, 1.5, (TOP, T)); g = g / g.sum(0)
    w1 = [pack_weight(m, "e2m1") for m in n((E, K, H)) / np.sqrt(K) / s[None] * u[None, None, :]]
    w2 = [pack_weight(m, "e2m1") for m in n((E, H, N)) / np.sqrt(H) / u[None, :, None]]
    x = pack_weight(n((K, T)) * s, "e4m3")
    return {
        "x_words": x[0],
        "x_scales": x[1],
        "w1_words": np.stack([m[0] for m in w1]),
        "w1_scales": np.stack([m[1] for m in w1]),
        "w2_words": np.stack([m[0] for m in w2]),
        "w2_scales": np.stack([m[1] for m in w2]),
        "gate": np.stack([np.tile(r, (N, 1)) for r in g]).astype(np.float32),
        "offs": striped(slot_token),
        "pos1": striped(pos[0]),
        "pos2": striped(pos[1]),
        "pos3": striped(pos[2]),
        "pos4": striped(pos[3]),
    }


def reference(x_words, x_scales, w1_words, w1_scales, w2_words, w2_scales, gate, offs, pos1, pos2, pos3, pos4):
    idx = unstriped(offs)
    w1 = np.stack([unpack_weight(w1_words[e], w1_scales[e], "e2m1") for e in range(E)])
    w2 = np.stack([unpack_weight(w2_words[e], w2_scales[e], "e2m1") for e in range(E)])
    xq = unpack_weight(x_words, x_scales, "e4m3")[:, idx]
    h = gelu(by_expert(w1, xq))
    y = by_expert(w2, mxq(h, 0, "e4m3"))
    return sum(f64(gate[r]) * y[:, unstriped(p)] for r, p in enumerate((pos1, pos2, pos3, pos4)))

@@ -1,0 +1,252 @@
+from contextlib import ExitStack
+
+import concourse.mybir as mybir
+from concourse.masks import make_identity
+
+K, T, E, C, H, N = 512, 512, 16, 128, 512, 384
+TOP = 4
+P = 128
+S = E * C
+FLOPS = 2 * S * (K * H + H * N)
+
+F32 = mybir.dt.float32
+BF16 = mybir.dt.bfloat16
+I32 = mybir.dt.int32
+U32 = mybir.dt.uint32
+U16 = mybir.dt.uint16
+U8 = mybir.dt.uint8
+FP8X4 = mybir.dt.float8_e4m3fn_x4
+FP4X4 = mybir.dt.float4_e2m1fn_x4
+ACT = mybir.ActivationFunctionType
+ALU = mybir.AluOpType
+
+GROUP = 4
+HALF = E // 2
+STARTS = (0, 4, 16)
+NB = N // P
+TB = T // P
+PATHS = ["aaaa", "aaaa", "aaav"]
+TURN_ON_VECTOR = {4,5,6}
+Y0_ON_VECTOR = {2,3}
+A_BANKS = (0, 1, 2)
+T_BANKS = (3, 4)
+Y0_BANKS = (5,6,3,4,6)
+Y12_BANKS = (0, 1)
+X_BANKS = (3, 4)
+SUM_BANKS = (5, 6, 7)
+
+
+def tile_moe_pkd_mlp_gelu_kernel(
+    tc, x_words, x_scales, w1_words, w1_scales, w2_words, w2_scales, gate, offs, pos1, pos2, pos3, pos4, out
+):
+    nc = tc.nc
+    with ExitStack() as ctx:
+        lists = ctx.enter_context(tc.tile_pool(name="lists", bufs=1))
+        keep = ctx.enter_context(tc.tile_pool(name="keep", bufs=1))
+        ring = ctx.enter_context(tc.tile_pool(name="ring", bufs=3))
+        psum = ctx.enter_context(tc.psum_pool(name="psum", bufs=1))
+
+        offs_t = lists.tile([P, S // 16], U16, name="offs_t")
+        pos_t = [lists.tile([P, T // 16], U16, name="pos_t%d" % r) for r in range(TOP)]
+        xw = keep.tile([P, T], I32, name="xw", align_bytes=64)
+        xs = keep.tile([P, T], U8, name="xs", align_bytes=64)
+        w1s = [keep.tile([P, (STARTS[i + 1] - STARTS[i]) * H], U8, name="w1s%d" % i, align_bytes=64) for i in range(len(STARTS) - 1)]
+        w2s = keep.tile([P, E * N], U8, name="w2s", align_bytes=64)
+        w1w = [keep.tile([P, GROUP * 2 * H], U8, name="w1w%d" % g, align_bytes=64) for g in range(E // GROUP)]
+        w2w = [keep.tile([P, HALF * 2 * N], U8, name="w2w%d" % i, align_bytes=64) for i in range(2)]
+        g_rows = keep.tile([P, P], F32, name="g_rows", align_bytes=64)
+        g_col = keep.tile([P, TOP * TB], F32, name="g_col", align_bytes=64)
+        ident = keep.tile([P, P], F32, name="ident", align_bytes=64)
+        warm = keep.tile([P, 2], F32, name="warm", align_bytes=64)
+        fused_r = sorted({r for b in range(NB) for r in range(TOP) if PATHS[b][r] != "a"})
+        g_full = {r: keep.tile([P, T], F32, name="g_full%d" % r, align_bytes=64) for r in fused_r}
+        banks = [psum.tile([P, T], F32, name="bank%d" % i) for i in range(8)]
+
+        def load_words(tile, words):
+            nc.sync.dma_start(
+                out=tile[:].bitcast(I32).rearrange("p (e c) -> p e c", e=words.shape[0]),
+                in_=words.rearrange("e p c -> p e c").bitcast(I32),
+            )
+
+        def load_plane(queue, plane, rows):
+            for r in range(4):
+                queue.dma_start(
+                    out=plane[r:P:32, :].bitcast(I32).rearrange("p (e c) -> p e c", e=rows.shape[0]),
+                    in_=rows[:, r:16:4, :].rearrange("e q c -> q e c").bitcast(I32),
+                )
+
+        nc.gpsimd.memset(xs[:].bitcast(I32), 0)
+        nc.gpsimd.memset(w1s[0][:].bitcast(I32), 0)
+        nc.vector.memset(warm[:, 0:1], 0.0)
+        for plane in w1s[1:]:
+            nc.vector.memset(plane[:].bitcast(I32), 0)
+        nc.gpsimd.memset(w2s[:].bitcast(I32), 0)
+        nc.gpsimd.memset(g_rows[:], 0.0)
+        nc.scalar.activation(out=warm[:, 1:2], in_=warm[:, 0:1], func=ACT.Gelu_apprx_tanh)
+
+        gate_runs = gate.rearrange("r n (b p) -> (r n b) p", p=P)
+        step = N + 1
+        nc.sync.dma_start(offs_t[:], offs)
+        nc.sync.dma_start(out=xw[:], in_=x_words[0].rearrange("p t r -> p (t r)").bitcast(I32))
+        load_plane(nc.sync, xs, x_scales)
+        load_words(w1w[0], w1_words[0:4, 0])
+        load_plane(nc.sync, w1s[0], w1_scales[0:4, 0])
+        load_words(w1w[1], w1_words[4:8, 0])
+        load_plane(nc.sync, w1s[1], w1_scales[4:16, 0])
+        load_words(w1w[2], w1_words[8:12, 0])
+        load_words(w1w[3], w1_words[12:16, 0])
+        load_plane(nc.sync, w2s, w2_scales[:, 0])
+        load_words(w2w[1], w2_words[HALF:E, 0])
+        load_words(w2w[0], w2_words[0:HALF, 0])
+        nc.sync.dma_start(out=g_rows[0 : TOP * TB, :], in_=gate_runs[0 : (TOP * TB - 1) * step + 1 : step, :])
+        for r, pos in enumerate((pos1, pos2, pos3, pos4)):
+            nc.sync.dma_start(pos_t[r][:], pos)
+        for r in fused_r:
+            nc.sync.dma_start(out=g_full[r][:], in_=gate[r, 0:P, :])
+        make_identity(nc, ident[:])
+
+        hq = [keep.tile([P, 2 * C], U32, name="hq%d" % q, align_bytes=64) for q in range(E // 2)]
+        hs = [keep.tile([P, 2 * C], U8, name="hs%d" % q, align_bytes=64) for q in range(E // 2)]
+        y = [keep.tile([P, S], F32, name="y%d" % b, align_bytes=64) for b in range(NB)]
+
+        def rows_of(b, e0, e1, bank, copy):
+            for e in range(e0, e1):
+                lo = (e % HALF) * N + b * P
+                cols = slice((e % 2) * C, (e % 2 + 1) * C)
+                nc.tensor.matmul_mx(
+                    out=bank[:, (e - e0) * C : (e - e0 + 1) * C],
+                    lhsT=w2w[e // HALF][:, 2 * lo : 2 * (lo + P)].bitcast(FP4X4),
+                    lhsT_scale=w2s[:, e * N + b * P : e * N + (b + 1) * P],
+                    rhs=hq[e // 2][:, cols].bitcast(FP8X4),
+                    rhs_scale=hs[e // 2][:, cols],
+                    start=True,
+                    stop=True,
+                )
+            copy(out=y[b][:, e0 * C : e1 * C], in_=bank[:, 0 : (e1 - e0) * C])
+
+        def gather_tokens(lo, n):
+            gw = ring.tile([P, 2 * C], U32, name="gw", tag="gw", bufs=2, align_bytes=64)
+            gs = ring.tile([P, 2 * C], U8, name="gs", tag="gs", bufs=2, align_bytes=64)
+            for a in range(0, 2 * C, n):
+                entries = offs_t[:, (lo + a) // 16 : (lo + a + n) // 16]
+                nc.vector.tensor_copy(out=gw[:, a : a + n], in_=xw[:].bitcast(U32).indirect(entries))
+                nc.vector.tensor_copy(out=gs[:, a : a + n], in_=xs[:].indirect(entries))
+            return gw, gs
+
+        def first_layer(e, gw, gs, h):
+            j = e % 2
+            a_bank = banks[A_BANKS[e % len(A_BANKS)]]
+            i = max(i for i in range(len(STARTS) - 1) if STARTS[i] <= e)
+            lo = e - STARTS[i]
+            nc.tensor.matmul_mx(
+                out=a_bank[:],
+                lhsT=gw[:, j * C : (j + 1) * C].bitcast(FP8X4),
+                lhsT_scale=gs[:, j * C : (j + 1) * C],
+                rhs=w1w[e // GROUP][:, (e % GROUP) * 2 * H : (e % GROUP + 1) * 2 * H].bitcast(FP4X4),
+                rhs_scale=w1s[i][:, lo * H : (lo + 1) * H],
+                start=True,
+                stop=True,
+            )
+            nc.scalar.activation(
+                out=h.rearrange("s (u p d) -> s u p d", u=2, d=2),
+                in_=a_bank[:].rearrange("s (p u d) -> s u p d", u=2, d=2),
+                func=ACT.Gelu_apprx_tanh,
+            )
+
+        def quantise(e0, n, h, bank, copy):
+            turned = bank[:, 0 : n * 2 * C].rearrange("p (j u s) -> p j u s", j=n, u=2)
+            for j in range(n):
+                for u in range(2):
+                    nc.tensor.transpose(turned[:, j, u, :], h[:].bitcast(F32)[:, j, u * P : (u + 1) * P], ident[:])
+            ht = ring.tile([P, n * H], BF16, name="ht", tag="ht", bufs=3, align_bytes=64)
+            copy(
+                out=ht[:].bitcast(F32).rearrange("p (j s u) -> p j s u", j=n, u=2),
+                in_=turned.rearrange("p j u s -> p j s u"),
+            )
+            cols = slice((e0 % 2) * C, (e0 % 2 + n) * C)
+            nc.vector.quantize_mx(out=hq[e0 // 2][:, cols].bitcast(FP8X4), scales=hs[e0 // 2][:, cols], in_=ht[:])
+
+        def y0_copy(g):
+            return nc.vector.tensor_copy if g in Y0_ON_VECTOR else nc.scalar.copy
+
+        for q in range(E // 2):
+            gw, gs = gather_tokens(2 * C * q, C if q == 0 else 2 * C)
+            if q < E // 2 - 1:
+                h = ring.tile([P, 2, H], BF16, name="h", tag="h", bufs=3, align_bytes=64)
+                for j in range(2):
+                    first_layer(2 * q + j, gw, gs, h[:, j, :])
+                quantise(2 * q, 2, h, banks[T_BANKS[q % len(T_BANKS)]], nc.vector.tensor_copy if q in TURN_ON_VECTOR else nc.scalar.copy)
+            else:
+                for e in (2 * q, 2 * q + 1):
+                    h = ring.tile([P, 1, H], BF16, name="h", tag="h", bufs=3, align_bytes=64)
+                    first_layer(e, gw, gs, h[:, 0, :])
+                    quantise(e, 1, h, banks[(4, 7)[e % 2]], nc.scalar.copy if e == 2 * q else nc.scalar.copy)
+        for g in range(E // GROUP - 1):
+            rows_of(0, GROUP * g, GROUP * (g + 1), banks[Y0_BANKS[g]], y0_copy(g))
+        rows_of(0, E - GROUP, E, banks[Y0_BANKS[3]], y0_copy(3))
+
+        g_bank = banks[2]
+        nc.tensor.transpose(g_bank[:, 0:P], g_rows[:], ident[:])
+        nc.scalar.copy(out=g_col[:], in_=g_bank[:, 0 : TOP * TB])
+
+        uses = []
+        for b in range(NB):
+            path = PATHS[b]
+            n_back = path.count("a") + (1 if "c" in path else 0)
+            total = banks[SUM_BANKS[b]]
+            result = ring.tile([P, T], F32, name="result", tag="result", bufs=3, align_bytes=64)
+            backs = []
+            summed = None
+            acc = total
+
+            def turn_back(weighed):
+                backs.append(weighed)
+                for k in range(TB):
+                    nc.tensor.matmul(
+                        total[:, k * P : (k + 1) * P], weighed[:, k, :], ident[:], is_transpose=True,
+                        start=(len(backs) == 1 and k == 0), stop=(len(backs) == n_back and k == TB - 1),
+                    )
+
+            def next_bank():
+                uses.append(0)
+                return banks[X_BANKS[(len(uses) - 1) % len(X_BANKS)]][:].rearrange("p (k n) -> p k n", k=TB)
+
+            for r in range(TOP):
+                for bb, g in {(0,0):((1,0),(1,1),(1,2),(1,3)),(0,2):((2,0),),(0,3):((2,1),),(1,0):((2,2),),(1,1):((2,3),)}.get((b, r), ()):
+                    rows_of(bb, GROUP * g, GROUP * (g + 1), banks[Y12_BANKS[g % len(Y12_BANKS)]], nc.scalar.copy)
+                picked = ring.tile([P, T], F32, name="picked", tag="picked", bufs=3, align_bytes=64)
+                if path[r] == "a":
+                    nc.vector.tensor_copy(out=picked[:], in_=y[b][:].indirect(pos_t[r][:]))
+                    across = next_bank()
+                    for k in range(TB):
+                        nc.tensor.transpose(across[:, k, :], picked[:, k * P : (k + 1) * P], ident[:])
+                    weighed = ring.tile([P, TB, P], F32, name="weighed", tag="weighed", bufs=2, align_bytes=64)
+                    for k in range(TB):
+                        nc.scalar.activation(
+                            out=weighed[:, k, :], in_=across[:, k, :], func=ACT.Copy,
+                            scale=g_col[:, r * TB + k : r * TB + k + 1],
+                        )
+                    turn_back(weighed)
+                    continue
+                nc.vector.tensor_tensor(picked[:], y[b][:].indirect(pos_t[r][:]), g_full[r][:], ALU.mult)
+                if path[r] == "c":
+                    first = "c" not in path[:r]
+                    last = "c" not in path[r + 1 :]
+                    if first:
+                        summed = next_bank()
+                    for k in range(TB):
+                        nc.tensor.matmul(
+                            summed[:, k, :], picked[:, k * P : (k + 1) * P], ident[:], is_transpose=True,
+                            start=(first and k == 0), stop=(last and k == TB - 1),
+                        )
+                    if last:
+                        weighed = ring.tile([P, TB, P], F32, name="weighed", tag="weighed", bufs=2, align_bytes=64)
+                        nc.scalar.copy(out=weighed[:], in_=summed)
+                        turn_back(weighed)
+                else:
+                    dst = result if r == TOP - 1 else ring.tile([P, T], F32, name="part", tag="part", bufs=2, align_bytes=64)
+                    nc.vector.tensor_tensor(dst[:], acc[:], picked[:], ALU.add)
+                    acc = dst
+            if "v" not in path:
+                nc.scalar.copy(out=result[:], in_=total[:])
+            nc.sync.dma_start(out=out[b * P : (b + 1) * P, :], in_=result[:])

@@ -23,23 +23,24 @@ ALU = mybir.AluOpType
 GROUP = 4
 HALF = E // 2
 STARTS = (0, 4, 16)
+WS = (0, 4, 8, 12, 16)
 NB = N // P
 TB = T // P
-PATHS = ["aaaa", "aaaa", "aaav"]
-TURN_ON_VECTOR = {4,5,6}
-Y0_ON_VECTOR = {2,3}
-A_BANKS = (0, 1, 2)
-T_BANKS = (3, 4)
-Y0_BANKS = (5,6,3,4,6)
-Y12_BANKS = (0, 1)
-X_BANKS = (3, 4)
-SUM_BANKS = (5, 6, 7)
+A_BANKS = 5
+LAG = 3
+HELD = 4
+VECTOR_FROM = 3
+Y12_BANKS = (5, 7)
+X_BANKS = (6, 0)
+SUM_BANKS = (1, 2, 3)
+ON_PE = 2
 
 
 def tile_moe_pkd_mlp_gelu_kernel(
     tc, x_words, x_scales, w1_words, w1_scales, w2_words, w2_scales, gate, offs, pos1, pos2, pos3, pos4, out
 ):
     nc = tc.nc
+    V_, S_ = nc.vector.tensor_copy, nc.scalar.copy
     with ExitStack() as ctx:
         lists = ctx.enter_context(tc.tile_pool(name="lists", bufs=1))
         keep = ctx.enter_context(tc.tile_pool(name="keep", bufs=1))
@@ -52,14 +53,11 @@ def tile_moe_pkd_mlp_gelu_kernel(
         xs = keep.tile([P, T], U8, name="xs", align_bytes=64)
         w1s = [keep.tile([P, (STARTS[i + 1] - STARTS[i]) * H], U8, name="w1s%d" % i, align_bytes=64) for i in range(len(STARTS) - 1)]
         w2s = keep.tile([P, E * N], U8, name="w2s", align_bytes=64)
-        w1w = [keep.tile([P, GROUP * 2 * H], U8, name="w1w%d" % g, align_bytes=64) for g in range(E // GROUP)]
+        w1w = [keep.tile([P, (WS[g + 1] - WS[g]) * 2 * H], U8, name="w1w%d" % g, align_bytes=64) for g in range(len(WS) - 1)]
         w2w = [keep.tile([P, HALF * 2 * N], U8, name="w2w%d" % i, align_bytes=64) for i in range(2)]
-        g_rows = keep.tile([P, P], F32, name="g_rows", align_bytes=64)
-        g_col = keep.tile([P, TOP * TB], F32, name="g_col", align_bytes=64)
         ident = keep.tile([P, P], F32, name="ident", align_bytes=64)
         warm = keep.tile([P, 2], F32, name="warm", align_bytes=64)
-        fused_r = sorted({r for b in range(NB) for r in range(TOP) if PATHS[b][r] != "a"})
-        g_full = {r: keep.tile([P, T], F32, name="g_full%d" % r, align_bytes=64) for r in fused_r}
+        g_full = [keep.tile([P, T], F32, name="g_full%d" % r, align_bytes=64) for r in range(TOP)]
         banks = [psum.tile([P, T], F32, name="bank%d" % i) for i in range(8)]
 
         def load_words(tile, words):
@@ -68,9 +66,9 @@ def tile_moe_pkd_mlp_gelu_kernel(
                 in_=words.rearrange("e p c -> p e c").bitcast(I32),
             )
 
-        def load_plane(queue, plane, rows):
+        def load_plane(plane, rows):
             for r in range(4):
-                queue.dma_start(
+                nc.sync.dma_start(
                     out=plane[r:P:32, :].bitcast(I32).rearrange("p (e c) -> p e c", e=rows.shape[0]),
                     in_=rows[:, r:16:4, :].rearrange("e q c -> q e c").bitcast(I32),
                 )
@@ -80,29 +78,29 @@ def tile_moe_pkd_mlp_gelu_kernel(
         nc.vector.memset(warm[:, 0:1], 0.0)
         for plane in w1s[1:]:
             nc.vector.memset(plane[:].bitcast(I32), 0)
-        nc.gpsimd.memset(w2s[:].bitcast(I32), 0)
-        nc.gpsimd.memset(g_rows[:], 0.0)
+        nc.vector.memset(w2s[:].bitcast(I32), 0)
         nc.scalar.activation(out=warm[:, 1:2], in_=warm[:, 0:1], func=ACT.Gelu_apprx_tanh)
 
-        gate_runs = gate.rearrange("r n (b p) -> (r n b) p", p=P)
-        step = N + 1
-        nc.sync.dma_start(offs_t[:], offs)
         nc.sync.dma_start(out=xw[:], in_=x_words[0].rearrange("p t r -> p (t r)").bitcast(I32))
-        load_plane(nc.sync, xs, x_scales)
+        load_plane(xs, x_scales)
+        nc.sync.dma_start(offs_t[:], offs)
         load_words(w1w[0], w1_words[0:4, 0])
-        load_plane(nc.sync, w1s[0], w1_scales[0:4, 0])
+        load_plane(w1s[0], w1_scales[0:4, 0])
         load_words(w1w[1], w1_words[4:8, 0])
-        load_plane(nc.sync, w1s[1], w1_scales[4:16, 0])
+        load_plane(w1s[1], w1_scales[4:16, 0])
         load_words(w1w[2], w1_words[8:12, 0])
         load_words(w1w[3], w1_words[12:16, 0])
-        load_plane(nc.sync, w2s, w2_scales[:, 0])
-        load_words(w2w[1], w2_words[HALF:E, 0])
         load_words(w2w[0], w2_words[0:HALF, 0])
-        nc.sync.dma_start(out=g_rows[0 : TOP * TB, :], in_=gate_runs[0 : (TOP * TB - 1) * step + 1 : step, :])
-        for r, pos in enumerate((pos1, pos2, pos3, pos4)):
-            nc.sync.dma_start(pos_t[r][:], pos)
-        for r in fused_r:
-            nc.sync.dma_start(out=g_full[r][:], in_=gate[r, 0:P, :])
+        load_words(w2w[1], w2_words[HALF:E, 0])
+        load_plane(w2s, w2_scales[:, 0])
+        nc.sync.dma_start(pos_t[0][:], pos1)
+        nc.sync.dma_start(out=g_full[0][:], in_=gate[0, 0:P, :])
+        nc.sync.dma_start(pos_t[1][:], pos2)
+        nc.sync.dma_start(out=g_full[1][:], in_=gate[1, 0:P, :])
+        nc.sync.dma_start(pos_t[2][:], pos3)
+        nc.sync.dma_start(out=g_full[2][:], in_=gate[2, 0:P, :])
+        nc.sync.dma_start(pos_t[3][:], pos4)
+        nc.sync.dma_start(out=g_full[3][:], in_=gate[3, 0:P, :])
         make_identity(nc, ident[:])
 
         hq = [keep.tile([P, 2 * C], U32, name="hq%d" % q, align_bytes=64) for q in range(E // 2)]
@@ -125,8 +123,8 @@ def tile_moe_pkd_mlp_gelu_kernel(
             copy(out=y[b][:, e0 * C : e1 * C], in_=bank[:, 0 : (e1 - e0) * C])
 
         def gather_tokens(lo, n):
-            gw = ring.tile([P, 2 * C], U32, name="gw", tag="gw", bufs=2, align_bytes=64)
-            gs = ring.tile([P, 2 * C], U8, name="gs", tag="gs", bufs=2, align_bytes=64)
+            gw = ring.tile([P, 2 * C], U32, name="gw", tag="gw", bufs=4, align_bytes=64)
+            gs = ring.tile([P, 2 * C], U8, name="gs", tag="gs", bufs=4, align_bytes=64)
             for a in range(0, 2 * C, n):
                 entries = offs_t[:, (lo + a) // 16 : (lo + a + n) // 16]
                 nc.vector.tensor_copy(out=gw[:, a : a + n], in_=xw[:].bitcast(U32).indirect(entries))
@@ -135,14 +133,15 @@ def tile_moe_pkd_mlp_gelu_kernel(
 
         def first_layer(e, gw, gs, h):
             j = e % 2
-            a_bank = banks[A_BANKS[e % len(A_BANKS)]]
+            a_bank = banks[e % A_BANKS]
             i = max(i for i in range(len(STARTS) - 1) if STARTS[i] <= e)
             lo = e - STARTS[i]
+            wg = max(i for i in range(len(WS) - 1) if WS[i] <= e)
             nc.tensor.matmul_mx(
                 out=a_bank[:],
                 lhsT=gw[:, j * C : (j + 1) * C].bitcast(FP8X4),
                 lhsT_scale=gs[:, j * C : (j + 1) * C],
-                rhs=w1w[e // GROUP][:, (e % GROUP) * 2 * H : (e % GROUP + 1) * 2 * H].bitcast(FP4X4),
+                rhs=w1w[wg][:, (e - WS[wg]) * 2 * H : (e - WS[wg] + 1) * 2 * H].bitcast(FP4X4),
                 rhs_scale=w1s[i][:, lo * H : (lo + 1) * H],
                 start=True,
                 stop=True,
@@ -158,7 +157,7 @@ def tile_moe_pkd_mlp_gelu_kernel(
             for j in range(n):
                 for u in range(2):
                     nc.tensor.transpose(turned[:, j, u, :], h[:].bitcast(F32)[:, j, u * P : (u + 1) * P], ident[:])
-            ht = ring.tile([P, n * H], BF16, name="ht", tag="ht", bufs=3, align_bytes=64)
+            ht = ring.tile([P, n * H], BF16, name="ht", tag="ht", bufs=4, align_bytes=64)
             copy(
                 out=ht[:].bitcast(F32).rearrange("p (j s u) -> p j s u", j=n, u=2),
                 in_=turned.rearrange("p j u s -> p j s u"),
@@ -166,87 +165,65 @@ def tile_moe_pkd_mlp_gelu_kernel(
             cols = slice((e0 % 2) * C, (e0 % 2 + n) * C)
             nc.vector.quantize_mx(out=hq[e0 // 2][:, cols].bitcast(FP8X4), scales=hs[e0 // 2][:, cols], in_=ht[:])
 
-        def y0_copy(g):
-            return nc.vector.tensor_copy if g in Y0_ON_VECTOR else nc.scalar.copy
+        hidden = {}
+        for e in range(E):
+            q, j = divmod(e, 2)
+            last = q == E // 2 - 1
+            if j == 0:
+                gw, gs = gather_tokens(2 * C * q, C if q == 0 else 2 * C)
+            if j == 0 or last:
+                h = ring.tile([P, 1 if last else 2, H], BF16, name="h", tag="h", bufs=6, align_bytes=64)
+                hidden[q] = h
+            first_layer(e, gw, gs, h[:, 0 if last else j, :])
+            for p in range(E // 2 - 1):
+                if e == (2 * p + 1 + LAG if p < HELD else 2 * p + 2):
+                    bank = banks[e % A_BANKS] if p < HELD else banks[5 + p % 2]
+                    quantise(2 * p, 2, hidden[p], bank, V_ if p >= VECTOR_FROM else S_)
+            if last:
+                quantise(e, 1, h, banks[(6, 7)[j]], S_ if j else S_)
+        for e0, e1, bank, copy in [(0, 4, 1, S_), (4, 8, 2, V_), (8, 12, 3, S_), (12, 15, 4, V_), (15, 16, 0, S_)]:
+            rows_of(0, e0, e1, banks[bank], copy)
 
-        for q in range(E // 2):
-            gw, gs = gather_tokens(2 * C * q, C if q == 0 else 2 * C)
-            if q < E // 2 - 1:
-                h = ring.tile([P, 2, H], BF16, name="h", tag="h", bufs=3, align_bytes=64)
-                for j in range(2):
-                    first_layer(2 * q + j, gw, gs, h[:, j, :])
-                quantise(2 * q, 2, h, banks[T_BANKS[q % len(T_BANKS)]], nc.vector.tensor_copy if q in TURN_ON_VECTOR else nc.scalar.copy)
-            else:
-                for e in (2 * q, 2 * q + 1):
-                    h = ring.tile([P, 1, H], BF16, name="h", tag="h", bufs=3, align_bytes=64)
-                    first_layer(e, gw, gs, h[:, 0, :])
-                    quantise(e, 1, h, banks[(4, 7)[e % 2]], nc.scalar.copy if e == 2 * q else nc.scalar.copy)
-        for g in range(E // GROUP - 1):
-            rows_of(0, GROUP * g, GROUP * (g + 1), banks[Y0_BANKS[g]], y0_copy(g))
-        rows_of(0, E - GROUP, E, banks[Y0_BANKS[3]], y0_copy(3))
+        pending = []
 
-        g_bank = banks[2]
-        nc.tensor.transpose(g_bank[:, 0:P], g_rows[:], ident[:])
-        nc.scalar.copy(out=g_col[:], in_=g_bank[:, 0 : TOP * TB])
+        def leave(b, result, total):
+            nc.scalar.copy(out=result[:], in_=total[:])
+            nc.sync.dma_start(out=out[b * P : (b + 1) * P, :], in_=result[:])
 
-        uses = []
         for b in range(NB):
-            path = PATHS[b]
-            n_back = path.count("a") + (1 if "c" in path else 0)
+            on_pe = ON_PE if b == NB - 1 else TOP
             total = banks[SUM_BANKS[b]]
+            summed = banks[X_BANKS[b % 2]][:].rearrange("p (k n) -> p k n", k=TB)
             result = ring.tile([P, T], F32, name="result", tag="result", bufs=3, align_bytes=64)
-            backs = []
-            summed = None
-            acc = total
-
-            def turn_back(weighed):
-                backs.append(weighed)
-                for k in range(TB):
-                    nc.tensor.matmul(
-                        total[:, k * P : (k + 1) * P], weighed[:, k, :], ident[:], is_transpose=True,
-                        start=(len(backs) == 1 and k == 0), stop=(len(backs) == n_back and k == TB - 1),
-                    )
-
-            def next_bank():
-                uses.append(0)
-                return banks[X_BANKS[(len(uses) - 1) % len(X_BANKS)]][:].rearrange("p (k n) -> p k n", k=TB)
-
+            rest = None
             for r in range(TOP):
                 for bb, g in {(0,0):((1,0),(1,1),(1,2),(1,3)),(0,2):((2,0),),(0,3):((2,1),),(1,0):((2,2),),(1,1):((2,3),)}.get((b, r), ()):
-                    rows_of(bb, GROUP * g, GROUP * (g + 1), banks[Y12_BANKS[g % len(Y12_BANKS)]], nc.scalar.copy)
-                picked = ring.tile([P, T], F32, name="picked", tag="picked", bufs=3, align_bytes=64)
-                if path[r] == "a":
-                    nc.vector.tensor_copy(out=picked[:], in_=y[b][:].indirect(pos_t[r][:]))
-                    across = next_bank()
-                    for k in range(TB):
-                        nc.tensor.transpose(across[:, k, :], picked[:, k * P : (k + 1) * P], ident[:])
-                    weighed = ring.tile([P, TB, P], F32, name="weighed", tag="weighed", bufs=2, align_bytes=64)
-                    for k in range(TB):
-                        nc.scalar.activation(
-                            out=weighed[:, k, :], in_=across[:, k, :], func=ACT.Copy,
-                            scale=g_col[:, r * TB + k : r * TB + k + 1],
-                        )
-                    turn_back(weighed)
-                    continue
+                    rows_of(bb, GROUP * g, GROUP * (g + 1), banks[Y12_BANKS[g % 2]], S_)
+                if r == 2 and pending:
+                    leave(*pending.pop())
+                picked = ring.tile([P, T], F32, name="picked", tag="picked", bufs=4, align_bytes=64)
                 nc.vector.tensor_tensor(picked[:], y[b][:].indirect(pos_t[r][:]), g_full[r][:], ALU.mult)
-                if path[r] == "c":
-                    first = "c" not in path[:r]
-                    last = "c" not in path[r + 1 :]
-                    if first:
-                        summed = next_bank()
+                if r < on_pe:
                     for k in range(TB):
                         nc.tensor.matmul(
                             summed[:, k, :], picked[:, k * P : (k + 1) * P], ident[:], is_transpose=True,
-                            start=(first and k == 0), stop=(last and k == TB - 1),
+                            start=(r == 0 and k == 0), stop=(r == on_pe - 1 and k == TB - 1),
                         )
-                    if last:
+                    if r == on_pe - 1:
                         weighed = ring.tile([P, TB, P], F32, name="weighed", tag="weighed", bufs=2, align_bytes=64)
                         nc.scalar.copy(out=weighed[:], in_=summed)
-                        turn_back(weighed)
+                        for k in range(TB):
+                            nc.tensor.transpose(total[:, k * P : (k + 1) * P], weighed[:, k, :], ident[:])
+                elif rest is None:
+                    rest = picked
                 else:
-                    dst = result if r == TOP - 1 else ring.tile([P, T], F32, name="part", tag="part", bufs=2, align_bytes=64)
-                    nc.vector.tensor_tensor(dst[:], acc[:], picked[:], ALU.add)
-                    acc = dst
-            if "v" not in path:
-                nc.scalar.copy(out=result[:], in_=total[:])
-            nc.sync.dma_start(out=out[b * P : (b + 1) * P, :], in_=result[:])
+                    part = ring.tile([P, T], F32, name="part", tag="part", bufs=2, align_bytes=64)
+                    nc.vector.tensor_tensor(part[:], rest[:], picked[:], ALU.add)
+                    rest = part
+            if rest is None:
+                pending.append((b, result, total))
+            else:
+                for lo in range(0, T, T // 2):
+                    cols = slice(lo, lo + T // 2)
+                    nc.vector.tensor_tensor(result[:, cols], total[:, cols], rest[:, cols], ALU.add)
+                    nc.sync.dma_start(out=out[b * P : (b + 1) * P, cols], in_=result[:, cols])

@@ -5,9 +5,7 @@ from concourse.masks import make_identity
 
 K, T, E, C, H, N = 512, 512, 16, 128, 512, 384
 TOP = 4
-P = 128
-S = E * C
-FLOPS = 2 * S * (K * H + H * N)
+FLOPS = 2 * E * C * (K * H + H * N)
 
 F32 = mybir.dt.float32
 BF16 = mybir.dt.bfloat16
@@ -17,47 +15,50 @@ U16 = mybir.dt.uint16
 U8 = mybir.dt.uint8
 FP8X4 = mybir.dt.float8_e4m3fn_x4
 FP4X4 = mybir.dt.float4_e2m1fn_x4
-ACT = mybir.ActivationFunctionType
-ALU = mybir.AluOpType
+GELU = mybir.ActivationFunctionType.Gelu_apprx_tanh
+MULT, ADD = mybir.AluOpType.mult, mybir.AluOpType.add
 
+P = 128
+SLOTS = E * C
+PAIRS = E // 2
 GROUP = 4
-HALF = E // 2
-STARTS = (0, 4, 16)
-WS = (0, 4, 8, 12, 16)
-NB = N // P
-TB = T // P
+GROUPS = E // GROUP
+BLOCKS = N // P
+TURNS = T // P
+PER_COLUMN = 16
+
+PLANE_STARTS = (0, GROUP, 2 * GROUP, E)
+
 A_BANKS = 5
+EARLY = 4
 LAG = 3
-HELD = 4
-VECTOR_FROM = 3
-Y12_BANKS = (5, 7)
-X_BANKS = (6, 0)
-SUM_BANKS = (1, 2, 3)
-ON_PE = 2
+ON_TENSOR = 2
 
 
 def tile_moe_pkd_mlp_gelu_kernel(
     tc, x_words, x_scales, w1_words, w1_scales, w2_words, w2_scales, gate, offs, pos1, pos2, pos3, pos4, out
 ):
     nc = tc.nc
-    V_, S_ = nc.vector.tensor_copy, nc.scalar.copy
+    vector_copy, scalar_copy = nc.vector.tensor_copy, nc.scalar.copy
     with ExitStack() as ctx:
         lists = ctx.enter_context(tc.tile_pool(name="lists", bufs=1))
         keep = ctx.enter_context(tc.tile_pool(name="keep", bufs=1))
-        ring = ctx.enter_context(tc.tile_pool(name="ring", bufs=3))
+        ring = ctx.enter_context(tc.tile_pool(name="ring", bufs=BLOCKS))
         psum = ctx.enter_context(tc.psum_pool(name="psum", bufs=1))
 
-        offs_t = lists.tile([P, S // 16], U16, name="offs_t")
-        pos_t = [lists.tile([P, T // 16], U16, name="pos_t%d" % r) for r in range(TOP)]
-        xw = keep.tile([P, T], I32, name="xw", align_bytes=64)
-        xs = keep.tile([P, T], U8, name="xs", align_bytes=64)
-        w1s = [keep.tile([P, (STARTS[i + 1] - STARTS[i]) * H], U8, name="w1s%d" % i, align_bytes=64) for i in range(len(STARTS) - 1)]
-        w2s = keep.tile([P, E * N], U8, name="w2s", align_bytes=64)
-        w1w = [keep.tile([P, (WS[g + 1] - WS[g]) * 2 * H], U8, name="w1w%d" % g, align_bytes=64) for g in range(len(WS) - 1)]
-        w2w = [keep.tile([P, HALF * 2 * N], U8, name="w2w%d" % i, align_bytes=64) for i in range(2)]
-        ident = keep.tile([P, P], F32, name="ident", align_bytes=64)
-        warm = keep.tile([P, 2], F32, name="warm", align_bytes=64)
-        g_full = [keep.tile([P, T], F32, name="g_full%d" % r, align_bytes=64) for r in range(TOP)]
+        def kept(name, width, dtype):
+            return keep.tile([P, width], dtype, name=name, align_bytes=64)
+
+        offs_t = lists.tile([P, SLOTS // PER_COLUMN], U16, name="offs_t")
+        pos_t = [lists.tile([P, T // PER_COLUMN], U16, name="pos_t%d" % r) for r in range(TOP)]
+        xw = kept("xw", T, I32)
+        xs = kept("xs", T, U8)
+        w1s = [kept("w1s%d" % i, (PLANE_STARTS[i + 1] - PLANE_STARTS[i]) * H, U8) for i in range(3)]
+        w2s = [kept("w2s%d" % b, E * P, U8) for b in range(BLOCKS)]
+        w1w = [kept("w1w%d" % g, GROUP * 2 * H, U8) for g in range(GROUPS)]
+        w2w = [kept("w2w%d" % b, E * 2 * P, U8) for b in range(BLOCKS)]
+        ident = kept("ident", P, F32)
+        gates = [kept("gates%d" % r, T, F32) for r in range(TOP)]
         banks = [psum.tile([P, T], F32, name="bank%d" % i) for i in range(8)]
 
         def load_words(tile, words):
@@ -70,160 +71,167 @@ def tile_moe_pkd_mlp_gelu_kernel(
             for r in range(4):
                 nc.sync.dma_start(
                     out=plane[r:P:32, :].bitcast(I32).rearrange("p (e c) -> p e c", e=rows.shape[0]),
-                    in_=rows[:, r:16:4, :].rearrange("e q c -> q e c").bitcast(I32),
+                    in_=rows[:, r:16:4, :].rearrange("e f c -> f e c").bitcast(I32),
                 )
 
-        nc.gpsimd.memset(xs[:].bitcast(I32), 0)
-        nc.gpsimd.memset(w1s[0][:].bitcast(I32), 0)
-        nc.vector.memset(warm[:, 0:1], 0.0)
-        for plane in w1s[1:]:
+        for plane in (xs, w1s[0]):
+            nc.gpsimd.memset(plane[:].bitcast(I32), 0)
+        for plane in w1s[1:] + w2s:
             nc.vector.memset(plane[:].bitcast(I32), 0)
-        nc.vector.memset(w2s[:].bitcast(I32), 0)
-        nc.scalar.activation(out=warm[:, 1:2], in_=warm[:, 0:1], func=ACT.Gelu_apprx_tanh)
 
         nc.sync.dma_start(out=xw[:], in_=x_words[0].rearrange("p t r -> p (t r)").bitcast(I32))
         load_plane(xs, x_scales)
         nc.sync.dma_start(offs_t[:], offs)
-        load_words(w1w[0], w1_words[0:4, 0])
-        load_plane(w1s[0], w1_scales[0:4, 0])
-        load_words(w1w[1], w1_words[4:8, 0])
-        load_plane(w1s[1], w1_scales[4:16, 0])
-        load_words(w1w[2], w1_words[8:12, 0])
-        load_words(w1w[3], w1_words[12:16, 0])
-        load_words(w2w[0], w2_words[0:HALF, 0])
-        load_words(w2w[1], w2_words[HALF:E, 0])
-        load_plane(w2s, w2_scales[:, 0])
-        nc.sync.dma_start(pos_t[0][:], pos1)
-        nc.sync.dma_start(out=g_full[0][:], in_=gate[0, 0:P, :])
-        nc.sync.dma_start(pos_t[1][:], pos2)
-        nc.sync.dma_start(out=g_full[1][:], in_=gate[1, 0:P, :])
-        nc.sync.dma_start(pos_t[2][:], pos3)
-        nc.sync.dma_start(out=g_full[2][:], in_=gate[2, 0:P, :])
-        nc.sync.dma_start(pos_t[3][:], pos4)
-        nc.sync.dma_start(out=g_full[3][:], in_=gate[3, 0:P, :])
+        for g in range(GROUPS):
+            load_words(w1w[g], w1_words[GROUP * g : GROUP * (g + 1), 0])
+            if g < len(w1s):
+                load_plane(w1s[g], w1_scales[PLANE_STARTS[g] : PLANE_STARTS[g + 1], 0])
+        for r, pos in enumerate((pos1, pos2, pos3, pos4)):
+            nc.sync.dma_start(pos_t[r][:], pos)
+        for b in range(BLOCKS):
+            load_words(w2w[b], w2_words[:, 0, :, 2 * b * P : 2 * (b + 1) * P])
+            load_plane(w2s[b], w2_scales[:, 0, :, b * P : (b + 1) * P])
+            for r in range(2 * b, min(2 * b + 2, TOP)):
+                nc.sync.dma_start(out=gates[r][:], in_=gate[r, 0:P, :])
         make_identity(nc, ident[:])
 
-        hq = [keep.tile([P, 2 * C], U32, name="hq%d" % q, align_bytes=64) for q in range(E // 2)]
-        hs = [keep.tile([P, 2 * C], U8, name="hs%d" % q, align_bytes=64) for q in range(E // 2)]
-        y = [keep.tile([P, S], F32, name="y%d" % b, align_bytes=64) for b in range(NB)]
+        hq = [kept("hq%d" % q, 2 * C, U32) for q in range(PAIRS)]
+        hs = [kept("hs%d" % q, 2 * C, U8) for q in range(PAIRS)]
+        y = [kept("y%d" % b, SLOTS, F32) for b in range(BLOCKS)]
 
-        def rows_of(b, e0, e1, bank, copy):
-            for e in range(e0, e1):
-                lo = (e % HALF) * N + b * P
-                cols = slice((e % 2) * C, (e % 2 + 1) * C)
-                nc.tensor.matmul_mx(
-                    out=bank[:, (e - e0) * C : (e - e0 + 1) * C],
-                    lhsT=w2w[e // HALF][:, 2 * lo : 2 * (lo + P)].bitcast(FP4X4),
-                    lhsT_scale=w2s[:, e * N + b * P : e * N + (b + 1) * P],
-                    rhs=hq[e // 2][:, cols].bitcast(FP8X4),
-                    rhs_scale=hs[e // 2][:, cols],
-                    start=True,
-                    stop=True,
-                )
-            copy(out=y[b][:, e0 * C : e1 * C], in_=bank[:, 0 : (e1 - e0) * C])
-
-        def gather_tokens(lo, n):
-            gw = ring.tile([P, 2 * C], U32, name="gw", tag="gw", bufs=4, align_bytes=64)
-            gs = ring.tile([P, 2 * C], U8, name="gs", tag="gs", bufs=4, align_bytes=64)
-            for a in range(0, 2 * C, n):
-                entries = offs_t[:, (lo + a) // 16 : (lo + a + n) // 16]
-                nc.vector.tensor_copy(out=gw[:, a : a + n], in_=xw[:].bitcast(U32).indirect(entries))
-                nc.vector.tensor_copy(out=gs[:, a : a + n], in_=xs[:].indirect(entries))
+        def gather_pair(q):
+            gw = ring.tile([P, 2 * C], U32, name="gw", bufs=4, align_bytes=64)
+            gs = ring.tile([P, 2 * C], U8, name="gs", bufs=4, align_bytes=64)
+            n = C if q == 0 else 2 * C
+            for lo in range(0, 2 * C, n):
+                first = (2 * C * q + lo) // PER_COLUMN
+                entries = offs_t[:, first : first + n // PER_COLUMN]
+                nc.vector.tensor_copy(out=gw[:, lo : lo + n], in_=xw[:].bitcast(U32).indirect(entries))
+                nc.vector.tensor_copy(out=gs[:, lo : lo + n], in_=xs[:].indirect(entries))
             return gw, gs
 
         def first_layer(e, gw, gs, h):
-            j = e % 2
-            a_bank = banks[e % A_BANKS]
-            i = max(i for i in range(len(STARTS) - 1) if STARTS[i] <= e)
-            lo = e - STARTS[i]
-            wg = max(i for i in range(len(WS) - 1) if WS[i] <= e)
+            bank = banks[e % A_BANKS]
+            slots = slice((e % 2) * C, (e % 2 + 1) * C)
+            part = min(e // GROUP, len(w1s) - 1)
+            at = e - PLANE_STARTS[part]
             nc.tensor.matmul_mx(
-                out=a_bank[:],
-                lhsT=gw[:, j * C : (j + 1) * C].bitcast(FP8X4),
-                lhsT_scale=gs[:, j * C : (j + 1) * C],
-                rhs=w1w[wg][:, (e - WS[wg]) * 2 * H : (e - WS[wg] + 1) * 2 * H].bitcast(FP4X4),
-                rhs_scale=w1s[i][:, lo * H : (lo + 1) * H],
+                out=bank[:],
+                lhsT=gw[:, slots].bitcast(FP8X4),
+                lhsT_scale=gs[:, slots],
+                rhs=w1w[e // GROUP][:, (e % GROUP) * 2 * H : (e % GROUP + 1) * 2 * H].bitcast(FP4X4),
+                rhs_scale=w1s[part][:, at * H : (at + 1) * H],
                 start=True,
                 stop=True,
             )
             nc.scalar.activation(
                 out=h.rearrange("s (u p d) -> s u p d", u=2, d=2),
-                in_=a_bank[:].rearrange("s (p u d) -> s u p d", u=2, d=2),
-                func=ACT.Gelu_apprx_tanh,
+                in_=bank[:].rearrange("s (p u d) -> s u p d", u=2, d=2),
+                func=GELU,
             )
 
-        def quantise(e0, n, h, bank, copy):
+        def turn_and_quantise(e0, n, h, bank, copy):
             turned = bank[:, 0 : n * 2 * C].rearrange("p (j u s) -> p j u s", j=n, u=2)
             for j in range(n):
                 for u in range(2):
                     nc.tensor.transpose(turned[:, j, u, :], h[:].bitcast(F32)[:, j, u * P : (u + 1) * P], ident[:])
-            ht = ring.tile([P, n * H], BF16, name="ht", tag="ht", bufs=4, align_bytes=64)
+            ht = ring.tile([P, n * H], BF16, name="ht", bufs=4, align_bytes=64)
             copy(
                 out=ht[:].bitcast(F32).rearrange("p (j s u) -> p j s u", j=n, u=2),
                 in_=turned.rearrange("p j u s -> p j s u"),
             )
-            cols = slice((e0 % 2) * C, (e0 % 2 + n) * C)
-            nc.vector.quantize_mx(out=hq[e0 // 2][:, cols].bitcast(FP8X4), scales=hs[e0 // 2][:, cols], in_=ht[:])
+            slots = slice((e0 % 2) * C, (e0 % 2 + n) * C)
+            nc.vector.quantize_mx(out=hq[e0 // 2][:, slots].bitcast(FP8X4), scales=hs[e0 // 2][:, slots], in_=ht[:])
 
-        hidden = {}
+        def second_layer(b, e0, e1, bank, copy):
+            for e in range(e0, e1):
+                slots = slice((e % 2) * C, (e % 2 + 1) * C)
+                nc.tensor.matmul_mx(
+                    out=bank[:, (e - e0) * C : (e - e0 + 1) * C],
+                    lhsT=w2w[b][:, 2 * e * P : 2 * (e + 1) * P].bitcast(FP4X4),
+                    lhsT_scale=w2s[b][:, e * P : (e + 1) * P],
+                    rhs=hq[e // 2][:, slots].bitcast(FP8X4),
+                    rhs_scale=hs[e // 2][:, slots],
+                    start=True,
+                    stop=True,
+                )
+            copy(out=y[b][:, e0 * C : e1 * C], in_=bank[:, 0 : (e1 - e0) * C])
+
+        hidden = []
         for e in range(E):
             q, j = divmod(e, 2)
-            last = q == E // 2 - 1
+            alone = q == PAIRS - 1
             if j == 0:
-                gw, gs = gather_tokens(2 * C * q, C if q == 0 else 2 * C)
-            if j == 0 or last:
-                h = ring.tile([P, 1 if last else 2, H], BF16, name="h", tag="h", bufs=6, align_bytes=64)
-                hidden[q] = h
-            first_layer(e, gw, gs, h[:, 0 if last else j, :])
-            for p in range(E // 2 - 1):
-                if e == (2 * p + 1 + LAG if p < HELD else 2 * p + 2):
-                    bank = banks[e % A_BANKS] if p < HELD else banks[5 + p % 2]
-                    quantise(2 * p, 2, hidden[p], bank, V_ if p >= VECTOR_FROM else S_)
-            if last:
-                quantise(e, 1, h, banks[(6, 7)[j]], S_ if j else S_)
-        for e0, e1, bank, copy in [(0, 4, 1, S_), (4, 8, 2, V_), (8, 12, 3, S_), (12, 15, 4, V_), (15, 16, 0, S_)]:
-            rows_of(0, e0, e1, banks[bank], copy)
+                gw, gs = gather_pair(q)
+            if j == 0 or alone:
+                hidden.append(ring.tile([P, 1 if alone else 2, H], BF16, name="h", bufs=6, align_bytes=64))
+            first_layer(e, gw, gs, hidden[-1][:, 0 if alone else j, :])
+            for pair in range(PAIRS - 1):
+                if pair < EARLY and e == 2 * pair + 1 + LAG:
+                    turn_and_quantise(2 * pair, 2, hidden[pair], banks[e % A_BANKS], scalar_copy)
+                if pair >= EARLY and e == 2 * pair + 2:
+                    turn_and_quantise(2 * pair, 2, hidden[pair], banks[A_BANKS + pair % 2], vector_copy)
+            if alone:
+                turn_and_quantise(e, 1, hidden[-1], banks[A_BANKS + 1 + j], scalar_copy)
 
-        pending = []
+        cuts = list(range(0, E, GROUP)) + [E - 1, E]
+        for i in range(len(cuts) - 1):
+            bank = banks[(E - A_BANKS + i) % A_BANKS]
+            second_layer(0, cuts[i], cuts[i + 1], bank, vector_copy if i % 2 else scalar_copy)
 
-        def leave(b, result, total):
-            nc.scalar.copy(out=result[:], in_=total[:])
+        row_banks = {1: (5, 6, 7, 1), 2: (2, 3, 4, 0)}
+        sum_banks = (row_banks[1][0], row_banks[2][0], row_banks[1][1])
+        back_banks = (row_banks[2][3], row_banks[1][3], row_banks[1][2])
+
+        def later_rows(b):
+            for g in range(GROUPS):
+                second_layer(b, GROUP * g, GROUP * (g + 1), banks[row_banks[b][g]], scalar_copy)
+
+        def leave(b, result):
+            nc.scalar.copy(out=result[:], in_=banks[back_banks[b]][:])
             nc.sync.dma_start(out=out[b * P : (b + 1) * P, :], in_=result[:])
 
-        for b in range(NB):
-            on_pe = ON_PE if b == NB - 1 else TOP
-            total = banks[SUM_BANKS[b]]
-            summed = banks[X_BANKS[b % 2]][:].rearrange("p (k n) -> p k n", k=TB)
-            result = ring.tile([P, T], F32, name="result", tag="result", bufs=3, align_bytes=64)
-            rest = None
+        results = []
+        for b in range(BLOCKS):
+            last = b == BLOCKS - 1
+            on_tensor = ON_TENSOR if last else TOP
+            summed = banks[sum_banks[b]][:].rearrange("t (k n) -> t k n", k=TURNS)
+            back = banks[back_banks[b]]
+            results.append(ring.tile([P, T], F32, name="result", align_bytes=64))
+            products = []
             for r in range(TOP):
-                for bb, g in {(0,0):((1,0),(1,1),(1,2),(1,3)),(0,2):((2,0),),(0,3):((2,1),),(1,0):((2,2),),(1,1):((2,3),)}.get((b, r), ()):
-                    rows_of(bb, GROUP * g, GROUP * (g + 1), banks[Y12_BANKS[g % 2]], S_)
-                if r == 2 and pending:
-                    leave(*pending.pop())
-                picked = ring.tile([P, T], F32, name="picked", tag="picked", bufs=4, align_bytes=64)
-                nc.vector.tensor_tensor(picked[:], y[b][:].indirect(pos_t[r][:]), g_full[r][:], ALU.mult)
-                if r < on_pe:
-                    for k in range(TB):
+                if b == 0 and r in (0, TOP - 1):
+                    later_rows(1 if r == 0 else 2)
+                if b > 0 and r == 2:
+                    leave(b - 1, results[b - 1])
+                product = ring.tile([P, T], F32, name="product", bufs=6, align_bytes=64)
+                products.append(product)
+                n = T // 2 if last and r == TOP - 1 else T
+                for lo in range(0, T, n):
+                    entries = pos_t[r][:, lo // PER_COLUMN : (lo + n) // PER_COLUMN]
+                    nc.vector.tensor_tensor(
+                        product[:, lo : lo + n], y[b][:].indirect(entries), gates[r][:, lo : lo + n], MULT
+                    )
+                if r < on_tensor:
+                    for k in range(TURNS):
                         nc.tensor.matmul(
-                            summed[:, k, :], picked[:, k * P : (k + 1) * P], ident[:], is_transpose=True,
-                            start=(r == 0 and k == 0), stop=(r == on_pe - 1 and k == TB - 1),
+                            summed[:, k, :],
+                            product[:, k * P : (k + 1) * P],
+                            ident[:],
+                            is_transpose=True,
+                            start=(r == 0 and k == 0),
+                            stop=(r == on_tensor - 1 and k == TURNS - 1),
                         )
-                    if r == on_pe - 1:
-                        weighed = ring.tile([P, TB, P], F32, name="weighed", tag="weighed", bufs=2, align_bytes=64)
-                        nc.scalar.copy(out=weighed[:], in_=summed)
-                        for k in range(TB):
-                            nc.tensor.transpose(total[:, k * P : (k + 1) * P], weighed[:, k, :], ident[:])
-                elif rest is None:
-                    rest = picked
-                else:
-                    part = ring.tile([P, T], F32, name="part", tag="part", bufs=2, align_bytes=64)
-                    nc.vector.tensor_tensor(part[:], rest[:], picked[:], ALU.add)
-                    rest = part
-            if rest is None:
-                pending.append((b, result, total))
-            else:
-                for lo in range(0, T, T // 2):
-                    cols = slice(lo, lo + T // 2)
-                    nc.vector.tensor_tensor(result[:, cols], total[:, cols], rest[:, cols], ALU.add)
-                    nc.sync.dma_start(out=out[b * P : (b + 1) * P, cols], in_=result[:, cols])
+                if r == on_tensor - 1:
+                    staged = ring.tile([P, TURNS, P], F32, name="staged", bufs=2, align_bytes=64)
+                    nc.scalar.copy(out=staged[:], in_=summed)
+                    for k in range(TURNS):
+                        nc.tensor.transpose(back[:, k * P : (k + 1) * P], staged[:, k, :], ident[:])
+
+        rest = ring.tile([P, T], F32, name="rest", bufs=1, align_bytes=64)
+        halves = (slice(0, T // 2), slice(T // 2, T))
+        for half in halves:
+            nc.vector.tensor_tensor(rest[:, half], products[ON_TENSOR][:, half], products[ON_TENSOR + 1][:, half], ADD)
+        for half in halves:
+            nc.vector.tensor_tensor(results[-1][:, half], back[:, half], rest[:, half], ADD)
+            nc.sync.dma_start(out=out[N - P : N, half], in_=results[-1][:, half])

from contextlib import ExitStack

import concourse.mybir as mybir
from concourse.masks import make_identity

K, T, E, C, H, N = 512, 512, 16, 128, 512, 384
TOP = 4
FLOPS = 2 * E * C * (K * H + H * N)

F32 = mybir.dt.float32
BF16 = mybir.dt.bfloat16
I32 = mybir.dt.int32
U32 = mybir.dt.uint32
U16 = mybir.dt.uint16
U8 = mybir.dt.uint8
FP8X4 = mybir.dt.float8_e4m3fn_x4
FP4X4 = mybir.dt.float4_e2m1fn_x4
GELU = mybir.ActivationFunctionType.Gelu_apprx_tanh
MULT, ADD = mybir.AluOpType.mult, mybir.AluOpType.add

P = 128
SLOTS = E * C
PAIRS = E // 2
GROUP = 4
GROUPS = E // GROUP
BLOCKS = N // P
TURNS = T // P
PER_COLUMN = 16

PLANE_STARTS = (0, GROUP, 2 * GROUP, E)

A_BANKS = 5
EARLY = 4
LAG = 3
ON_TENSOR = 2


def tile_moe_pkd_mlp_gelu_kernel(
    tc, x_words, x_scales, w1_words, w1_scales, w2_words, w2_scales, gate, offs, pos1, pos2, pos3, pos4, out
):
    nc = tc.nc
    vector_copy, scalar_copy = nc.vector.tensor_copy, nc.scalar.copy
    with ExitStack() as ctx:
        lists = ctx.enter_context(tc.tile_pool(name="lists", bufs=1))
        keep = ctx.enter_context(tc.tile_pool(name="keep", bufs=1))
        ring = ctx.enter_context(tc.tile_pool(name="ring", bufs=BLOCKS))
        psum = ctx.enter_context(tc.psum_pool(name="psum", bufs=1))

        def kept(name, width, dtype):
            return keep.tile([P, width], dtype, name=name, align_bytes=64)

        offs_t = lists.tile([P, SLOTS // PER_COLUMN], U16, name="offs_t")
        pos_t = [lists.tile([P, T // PER_COLUMN], U16, name="pos_t%d" % r) for r in range(TOP)]
        xw = kept("xw", T, I32)
        xs = kept("xs", T, U8)
        w1s = [kept("w1s%d" % i, (PLANE_STARTS[i + 1] - PLANE_STARTS[i]) * H, U8) for i in range(3)]
        w2s = [kept("w2s%d" % b, E * P, U8) for b in range(BLOCKS)]
        w1w = [kept("w1w%d" % g, GROUP * 2 * H, U8) for g in range(GROUPS)]
        w2w = [kept("w2w%d" % b, E * 2 * P, U8) for b in range(BLOCKS)]
        ident = kept("ident", P, F32)
        gates = [kept("gates%d" % r, T, F32) for r in range(TOP)]
        banks = [psum.tile([P, T], F32, name="bank%d" % i) for i in range(8)]

        def load_words(tile, words):
            nc.sync.dma_start(
                out=tile[:].bitcast(I32).rearrange("p (e c) -> p e c", e=words.shape[0]),
                in_=words.rearrange("e p c -> p e c").bitcast(I32),
            )

        def load_plane(plane, rows):
            for r in range(4):
                nc.sync.dma_start(
                    out=plane[r:P:32, :].bitcast(I32).rearrange("p (e c) -> p e c", e=rows.shape[0]),
                    in_=rows[:, r:16:4, :].rearrange("e f c -> f e c").bitcast(I32),
                )

        for plane in (xs, w1s[0]):
            nc.gpsimd.memset(plane[:].bitcast(I32), 0)
        for plane in w1s[1:] + w2s:
            nc.vector.memset(plane[:].bitcast(I32), 0)

        nc.sync.dma_start(out=xw[:], in_=x_words[0].rearrange("p t r -> p (t r)").bitcast(I32))
        load_plane(xs, x_scales)
        nc.sync.dma_start(offs_t[:], offs)
        for g in range(GROUPS):
            load_words(w1w[g], w1_words[GROUP * g : GROUP * (g + 1), 0])
            if g < len(w1s):
                load_plane(w1s[g], w1_scales[PLANE_STARTS[g] : PLANE_STARTS[g + 1], 0])
        for r, pos in enumerate((pos1, pos2, pos3, pos4)):
            nc.sync.dma_start(pos_t[r][:], pos)
        for b in range(BLOCKS):
            load_words(w2w[b], w2_words[:, 0, :, 2 * b * P : 2 * (b + 1) * P])
            load_plane(w2s[b], w2_scales[:, 0, :, b * P : (b + 1) * P])
            for r in range(2 * b, min(2 * b + 2, TOP)):
                nc.sync.dma_start(out=gates[r][:], in_=gate[r, 0:P, :])
        make_identity(nc, ident[:])

        hq = [kept("hq%d" % q, 2 * C, U32) for q in range(PAIRS)]
        hs = [kept("hs%d" % q, 2 * C, U8) for q in range(PAIRS)]
        y = [kept("y%d" % b, SLOTS, F32) for b in range(BLOCKS)]

        def gather_pair(q):
            gw = ring.tile([P, 2 * C], U32, name="gw", bufs=4, align_bytes=64)
            gs = ring.tile([P, 2 * C], U8, name="gs", bufs=4, align_bytes=64)
            n = C if q == 0 else 2 * C
            for lo in range(0, 2 * C, n):
                first = (2 * C * q + lo) // PER_COLUMN
                entries = offs_t[:, first : first + n // PER_COLUMN]
                nc.vector.tensor_copy(out=gw[:, lo : lo + n], in_=xw[:].bitcast(U32).indirect(entries))
                nc.vector.tensor_copy(out=gs[:, lo : lo + n], in_=xs[:].indirect(entries))
            return gw, gs

        def first_layer(e, gw, gs, h):
            bank = banks[e % A_BANKS]
            slots = slice((e % 2) * C, (e % 2 + 1) * C)
            part = min(e // GROUP, len(w1s) - 1)
            at = e - PLANE_STARTS[part]
            nc.tensor.matmul_mx(
                out=bank[:],
                lhsT=gw[:, slots].bitcast(FP8X4),
                lhsT_scale=gs[:, slots],
                rhs=w1w[e // GROUP][:, (e % GROUP) * 2 * H : (e % GROUP + 1) * 2 * H].bitcast(FP4X4),
                rhs_scale=w1s[part][:, at * H : (at + 1) * H],
                start=True,
                stop=True,
            )
            nc.scalar.activation(
                out=h.rearrange("s (u p d) -> s u p d", u=2, d=2),
                in_=bank[:].rearrange("s (p u d) -> s u p d", u=2, d=2),
                func=GELU,
            )

        def turn_and_quantise(e0, n, h, bank, copy):
            turned = bank[:, 0 : n * 2 * C].rearrange("p (j u s) -> p j u s", j=n, u=2)
            for j in range(n):
                for u in range(2):
                    nc.tensor.transpose(turned[:, j, u, :], h[:].bitcast(F32)[:, j, u * P : (u + 1) * P], ident[:])
            ht = ring.tile([P, n * H], BF16, name="ht", bufs=4, align_bytes=64)
            copy(
                out=ht[:].bitcast(F32).rearrange("p (j s u) -> p j s u", j=n, u=2),
                in_=turned.rearrange("p j u s -> p j s u"),
            )
            slots = slice((e0 % 2) * C, (e0 % 2 + n) * C)
            nc.vector.quantize_mx(out=hq[e0 // 2][:, slots].bitcast(FP8X4), scales=hs[e0 // 2][:, slots], in_=ht[:])

        def second_layer(b, e0, e1, bank, copy):
            for e in range(e0, e1):
                slots = slice((e % 2) * C, (e % 2 + 1) * C)
                nc.tensor.matmul_mx(
                    out=bank[:, (e - e0) * C : (e - e0 + 1) * C],
                    lhsT=w2w[b][:, 2 * e * P : 2 * (e + 1) * P].bitcast(FP4X4),
                    lhsT_scale=w2s[b][:, e * P : (e + 1) * P],
                    rhs=hq[e // 2][:, slots].bitcast(FP8X4),
                    rhs_scale=hs[e // 2][:, slots],
                    start=True,
                    stop=True,
                )
            copy(out=y[b][:, e0 * C : e1 * C], in_=bank[:, 0 : (e1 - e0) * C])

        hidden = []
        for e in range(E):
            q, j = divmod(e, 2)
            alone = q == PAIRS - 1
            if j == 0:
                gw, gs = gather_pair(q)
            if j == 0 or alone:
                hidden.append(ring.tile([P, 1 if alone else 2, H], BF16, name="h", bufs=6, align_bytes=64))
            first_layer(e, gw, gs, hidden[-1][:, 0 if alone else j, :])
            for pair in range(PAIRS - 1):
                if pair < EARLY and e == 2 * pair + 1 + LAG:
                    turn_and_quantise(2 * pair, 2, hidden[pair], banks[e % A_BANKS], scalar_copy)
                if pair >= EARLY and e == 2 * pair + 2:
                    turn_and_quantise(2 * pair, 2, hidden[pair], banks[A_BANKS + pair % 2], vector_copy)
            if alone:
                turn_and_quantise(e, 1, hidden[-1], banks[A_BANKS + 1 + j], scalar_copy)

        cuts = list(range(0, E, GROUP)) + [E - 1, E]
        for i in range(len(cuts) - 1):
            bank = banks[(E - A_BANKS + i) % A_BANKS]
            second_layer(0, cuts[i], cuts[i + 1], bank, vector_copy if i % 2 else scalar_copy)

        row_banks = {1: (5, 6, 7, 1), 2: (2, 3, 4, 0)}
        sum_banks = (row_banks[1][0], row_banks[2][0], row_banks[1][1])
        back_banks = (row_banks[2][3], row_banks[1][3], row_banks[1][2])

        def later_rows(b):
            for g in range(GROUPS):
                second_layer(b, GROUP * g, GROUP * (g + 1), banks[row_banks[b][g]], scalar_copy)

        def leave(b, result):
            nc.scalar.copy(out=result[:], in_=banks[back_banks[b]][:])
            nc.sync.dma_start(out=out[b * P : (b + 1) * P, :], in_=result[:])

        results = []
        for b in range(BLOCKS):
            last = b == BLOCKS - 1
            on_tensor = ON_TENSOR if last else TOP
            summed = banks[sum_banks[b]][:].rearrange("t (k n) -> t k n", k=TURNS)
            back = banks[back_banks[b]]
            results.append(ring.tile([P, T], F32, name="result", align_bytes=64))
            products = []
            for r in range(TOP):
                if b == 0 and r in (0, TOP - 1):
                    later_rows(1 if r == 0 else 2)
                if b > 0 and r == 2:
                    leave(b - 1, results[b - 1])
                product = ring.tile([P, T], F32, name="product", bufs=6, align_bytes=64)
                products.append(product)
                n = T // 2 if last and r == TOP - 1 else T
                for lo in range(0, T, n):
                    entries = pos_t[r][:, lo // PER_COLUMN : (lo + n) // PER_COLUMN]
                    nc.vector.tensor_tensor(
                        product[:, lo : lo + n], y[b][:].indirect(entries), gates[r][:, lo : lo + n], MULT
                    )
                if r < on_tensor:
                    for k in range(TURNS):
                        nc.tensor.matmul(
                            summed[:, k, :],
                            product[:, k * P : (k + 1) * P],
                            ident[:],
                            is_transpose=True,
                            start=(r == 0 and k == 0),
                            stop=(r == on_tensor - 1 and k == TURNS - 1),
                        )
                if r == on_tensor - 1:
                    staged = ring.tile([P, TURNS, P], F32, name="staged", bufs=2, align_bytes=64)
                    nc.scalar.copy(out=staged[:], in_=summed)
                    for k in range(TURNS):
                        nc.tensor.transpose(back[:, k * P : (k + 1) * P], staged[:, k, :], ident[:])

        rest = ring.tile([P, T], F32, name="rest", bufs=1, align_bytes=64)
        halves = (slice(0, T // 2), slice(T // 2, T))
        for half in halves:
            nc.vector.tensor_tensor(rest[:, half], products[ON_TENSOR][:, half], products[ON_TENSOR + 1][:, half], ADD)
        for half in halves:
            nc.vector.tensor_tensor(results[-1][:, half], back[:, half], rest[:, half], ADD)
            nc.sync.dma_start(out=out[N - P : N, half], in_=results[-1][:, half])
